import numpy as np
import ml_dtypes

BF16 = ml_dtypes.bfloat16


def bf(x):
    return np.asarray(x, np.float32).astype(BF16)


def f32(x):
    return np.asarray(x, np.float32)


def f64(x):
    return np.asarray(x).astype(np.float64)


def striped(idx):
    return np.tile(idx.reshape(-1, 16).T, (8, 1))


S, K, M, N, D = 512, 256, 128, 256, 256


def setup_inputs():
    return {"table": bf(np.random.standard_normal((K, S))), "qw": bf(np.random.standard_normal((K, M)) / np.sqrt(K)), "kw": bf(np.random.standard_normal((K, M)) / np.sqrt(K)), "w": bf(np.random.standard_normal((K, D)) / np.sqrt(K)), "r": f32(0.5 * np.random.standard_normal((1, N))), "offs": striped(np.random.permutation(S)[:N])}


def reference(table, qw, kw, w, r, offs):
    idx = offs[:16].T.reshape(-1)
    x = f64(table)[:, idx]
    a = (f64(qw).T @ x).T @ (f64(kw).T @ x) / np.sqrt(M) + f64(r)
    a = np.exp(a - a.max(axis=1, keepdims=True))
    a = a / a.sum(axis=1, keepdims=True)
    return a @ (f64(w).T @ x).T

@@ -1,0 +1,101 @@
+import math
+
+import concourse.mybir as mybir
+from concourse.masks import make_identity
+
+P = 128
+S, K, M, N, D = 512, 256, 128, 256, 256
+KB, NB, DB = K // P, N // P, D // P
+LANES = 16
+FLOPS = 2 * K * N * (2 * M + D) + 2 * N * N * (M + D)
+BYTES = 2 * K * N + 2 * K * (2 * M + D) + 4 * N + 2 * P * (N // LANES) + 4 * N * D
+
+BF16, F32, U16 = mybir.dt.bfloat16, mybir.dt.float32, mybir.dt.uint16
+ALU = mybir.AluOpType
+ACT = mybir.ActivationFunctionType
+
+
+def block(b):
+    return slice(b * P, (b + 1) * P)
+
+
+def tile_rows_pruneattn_sub_kernel(tc, table, qw, kw, w, r, offs, out):
+    nc = tc.nc
+    with (
+        tc.tile_pool(name="held", bufs=1) as held,
+        tc.tile_pool(name="work", bufs=NB) as work,
+        tc.psum_pool(name="psum", bufs=2) as psum,
+    ):
+        tokens = held.tile([P, KB, S], BF16, name="tokens")
+        qw_sb = held.tile([P, KB, M], BF16, name="qw_sb")
+        kw_sb = held.tile([P, KB, M], BF16, name="kw_sb")
+        w_sb = held.tile([P, KB, D], BF16, name="w_sb")
+        offsets = held.tile([P, N // LANES], U16, name="offsets")
+        bias = held.tile([P, N], F32, name="bias")
+        nc.sync.dma_start(offsets[:], offs)
+        nc.sync.dma_start(tokens[:], table.rearrange("(p a) s -> p a s", a=KB))
+        nc.scalar.dma_start(qw_sb[:], qw.rearrange("(p a) m -> p a m", a=KB))
+        nc.scalar.dma_start(kw_sb[:], kw.rearrange("(p a) m -> p a m", a=KB))
+        nc.sync.dma_start(w_sb[:], w.rearrange("(p a) d -> p a d", a=KB))
+        nc.scalar.dma_start(bias[:], r[0].partition_broadcast(P))
+
+        warm = held.tile([P, 1], F32, name="warm")
+        nc.vector.memset(warm[:], 0.0)
+        nc.scalar.activation(warm[:], warm[:], ACT.Exp)
+
+        identity = held.tile([P, P], BF16, name="identity")
+        make_identity(nc, identity[:])
+
+        def project(weights, columns, name, tag):
+            bank = psum.tile([P, N], F32, name=name, tag=tag)
+            for a in range(KB):
+                nc.tensor.matmul(bank[:], weights[:, a, columns], tokens[:, a, :].indirect(offsets[:]),
+                                 start=(a == 0), stop=(a == KB - 1))
+            return bank
+
+        q_ps = project(qw_sb, block(0), "q_ps", "qk_then_p")
+        h_ps = project(kw_sb, block(0), "h_ps", "qk_then_p")
+        v_ps = [project(w_sb, block(d), f"v_ps{d}", "v_then_out") for d in range(DB)]
+
+        q_sb = held.tile([P, N], BF16, name="q_sb")
+        h_sb = held.tile([P, N], BF16, name="h_sb")
+        nc.vector.tensor_copy(q_sb[:], q_ps[:])
+        nc.vector.tensor_copy(h_sb[:], h_ps[:])
+
+        scores = [psum.tile([P, N], F32, name=f"scores{i}", tag="scores") for i in range(NB)]
+        for i in range(NB):
+            nc.tensor.matmul(scores[i][:], q_sb[:, block(i)], h_sb[:], start=True, stop=True)
+
+        vt_sb = held.tile([P, NB, D], BF16, name="vt_sb")
+        for d in range(DB):
+            v_sb = work.tile([P, N], BF16, name="v_sb")
+            nc.scalar.copy(v_sb[:], v_ps[d][:])
+            vt_ps = psum.tile([P, NB, P], BF16, name="vt_ps")
+            for j in range(NB):
+                nc.tensor.transpose(vt_ps[:, j, :], v_sb[:, block(j)], identity[:])
+            nc.scalar.copy(vt_sb[:, :, block(d)], vt_ps[:])
+
+        for i in range(NB):
+            negated = work.tile([P, N], F32, name="negated")
+            nc.vector.scalar_tensor_tensor(negated[:], scores[i][:], -1.0 / math.sqrt(M), bias[:],
+                                           ALU.mult, ALU.subtract)
+            least = work.tile([P, 1], F32, name="least")
+            nc.vector.tensor_reduce(least[:], negated[:], mybir.AxisListType.X, ALU.min)
+            p_sb = work.tile([P, N], BF16, name="p_sb")
+            total = work.tile([P, 1], F32, name="total")
+            nc.scalar.activation(p_sb[:], negated[:], ACT.Exp, bias=least[:], scale=-1.0, accum_out=total[:])
+            inverse = work.tile([P, 1], F32, name="inverse")
+            nc.vector.reciprocal(inverse[:], total[:])
+
+            pt_ps = psum.tile([P, NB, P], BF16, name="pt_ps", tag="qk_then_p")
+            for j in range(NB):
+                nc.tensor.transpose(pt_ps[:, j, :], p_sb[:, block(j)], identity[:])
+            pt_sb = work.tile([P, NB, P], BF16, name="pt_sb")
+            nc.vector.tensor_copy(pt_sb[:], pt_ps[:])
+
+            out_ps = psum.tile([P, D], F32, name="out_ps", tag="v_then_out")
+            for j in range(NB):
+                nc.tensor.matmul(out_ps[:], pt_sb[:, j, :], vt_sb[:, j, :], start=(j == 0), stop=(j == NB - 1))
+            out_sb = work.tile([P, D], F32, name="out_sb")
+            nc.vector.tensor_scalar(out_sb[:], out_ps[:], inverse[:], None, ALU.mult)
+            nc.sync.dma_start(out[block(i), :], out_sb[:])

@@ -31,20 +31,28 @@ def tile_rows_pruneattn_sub_kernel(tc, table, qw, kw, w, r, offs, out):
         kw_sb = held.tile([P, KB, M], BF16, name="kw_sb")
         w_sb = held.tile([P, KB, D], BF16, name="w_sb")
         offsets = held.tile([P, N // LANES], U16, name="offsets")
-        bias = held.tile([P, N], F32, name="bias")
+        bias = held.tile([P, NB], F32, name="bias")
         nc.sync.dma_start(offsets[:], offs)
         nc.sync.dma_start(tokens[:], table.rearrange("(p a) s -> p a s", a=KB))
+        nc.scalar.dma_start(bias[:], r.rearrange("o (j p) -> p (o j)", p=P))
         nc.scalar.dma_start(qw_sb[:], qw.rearrange("(p a) m -> p a m", a=KB))
         nc.scalar.dma_start(kw_sb[:], kw.rearrange("(p a) m -> p a m", a=KB))
         nc.sync.dma_start(w_sb[:], w.rearrange("(p a) d -> p a d", a=KB))
-        nc.scalar.dma_start(bias[:], r[0].partition_broadcast(P))
 
         warm = held.tile([P, 1], F32, name="warm")
         nc.vector.memset(warm[:], 0.0)
         nc.scalar.activation(warm[:], warm[:], ACT.Exp)
 
+        identity32 = held.tile([P, P], F32, name="identity32")
+        make_identity(nc, identity32[:])
         identity = held.tile([P, P], BF16, name="identity")
-        make_identity(nc, identity[:])
+        nc.vector.tensor_copy(identity[:], identity32[:])
+
+        scores = [psum.tile([P, N], F32, name=f"scores{i}", tag="scores") for i in range(NB)]
+        for i in range(NB):
+            for j in range(NB):
+                nc.tensor.matmul(scores[i][:, block(j)], bias[:, j:j + 1].to_broadcast([P, P]), identity32[:],
+                                 start=(j == 0), stop=False, is_transpose=True)
 
         def project(weights, columns, name, tag):
             bank = psum.tile([P, N], F32, name=name, tag=tag)
@@ -59,12 +67,17 @@ def tile_rows_pruneattn_sub_kernel(tc, table, qw, kw, w, r, offs, out):
 
         q_sb = held.tile([P, N], BF16, name="q_sb")
         h_sb = held.tile([P, N], BF16, name="h_sb")
-        nc.vector.tensor_copy(q_sb[:], q_ps[:])
+        nc.vector.tensor_scalar(q_sb[:], q_ps[:], 1.0 / math.sqrt(M), None, ALU.mult)
         nc.vector.tensor_copy(h_sb[:], h_ps[:])
 
-        scores = [psum.tile([P, N], F32, name=f"scores{i}", tag="scores") for i in range(NB)]
         for i in range(NB):
-            nc.tensor.matmul(scores[i][:], q_sb[:, block(i)], h_sb[:], start=True, stop=True)
+            nc.tensor.matmul(scores[i][:], q_sb[:, block(i)], h_sb[:], start=False, stop=True)
+
+        shifts = []
+        for i in range(NB):
+            shift = work.tile([P, 1], F32, name="shift")
+            nc.vector.tensor_reduce(shift[:], scores[i][:], mybir.AxisListType.X, ALU.max, negate=True)
+            shifts.append(shift)
 
         vt_sb = held.tile([P, NB, D], BF16, name="vt_sb")
         for d in range(DB):
@@ -73,17 +86,12 @@ def tile_rows_pruneattn_sub_kernel(tc, table, qw, kw, w, r, offs, out):
             vt_ps = psum.tile([P, NB, P], BF16, name="vt_ps")
             for j in range(NB):
                 nc.tensor.transpose(vt_ps[:, j, :], v_sb[:, block(j)], identity[:])
-            nc.scalar.copy(vt_sb[:, :, block(d)], vt_ps[:])
+            nc.vector.tensor_copy(vt_sb[:, :, block(d)], vt_ps[:])
 
         for i in range(NB):
-            negated = work.tile([P, N], F32, name="negated")
-            nc.vector.scalar_tensor_tensor(negated[:], scores[i][:], -1.0 / math.sqrt(M), bias[:],
-                                           ALU.mult, ALU.subtract)
-            least = work.tile([P, 1], F32, name="least")
-            nc.vector.tensor_reduce(least[:], negated[:], mybir.AxisListType.X, ALU.min)
             p_sb = work.tile([P, N], BF16, name="p_sb")
             total = work.tile([P, 1], F32, name="total")
-            nc.scalar.activation(p_sb[:], negated[:], ACT.Exp, bias=least[:], scale=-1.0, accum_out=total[:])
+            nc.scalar.activation(p_sb[:], scores[i][:], ACT.Exp, bias=shifts[i][:], accum_out=total[:])
             inverse = work.tile([P, 1], F32, name="inverse")
             nc.vector.reciprocal(inverse[:], total[:])
 
@@ -91,11 +99,16 @@ def tile_rows_pruneattn_sub_kernel(tc, table, qw, kw, w, r, offs, out):
             for j in range(NB):
                 nc.tensor.transpose(pt_ps[:, j, :], p_sb[:, block(j)], identity[:])
             pt_sb = work.tile([P, NB, P], BF16, name="pt_sb")
-            nc.vector.tensor_copy(pt_sb[:], pt_ps[:])
-
             out_ps = psum.tile([P, D], F32, name="out_ps", tag="v_then_out")
+            out_sb = work.tile([P, D], F32, name="out_sb")
+            if i % 2 == 0:
+                nc.vector.tensor_copy(pt_sb[:], pt_ps[:])
+            else:
+                nc.scalar.copy(pt_sb[:], pt_ps[:])
             for j in range(NB):
                 nc.tensor.matmul(out_ps[:], pt_sb[:, j, :], vt_sb[:, j, :], start=(j == 0), stop=(j == NB - 1))
-            out_sb = work.tile([P, D], F32, name="out_sb")
-            nc.vector.tensor_scalar(out_sb[:], out_ps[:], inverse[:], None, ALU.mult)
+            if i % 2 == 0:
+                nc.vector.tensor_scalar(out_sb[:], out_ps[:], inverse[:], None, ALU.mult)
+            else:
+                nc.scalar.activation(out_sb[:], out_ps[:], ACT.Copy, scale=inverse[:])
             nc.sync.dma_start(out[block(i), :], out_sb[:])

@@ -43,6 +43,12 @@ def tile_rows_pruneattn_sub_kernel(tc, table, qw, kw, w, r, offs, out):
         nc.vector.memset(warm[:], 0.0)
         nc.scalar.activation(warm[:], warm[:], ACT.Exp)
 
+        zeros = held.tile([P, N], BF16, name="zeros")
+        nc.gpsimd.memset(zeros[:], 0.0)
+        idle_ps = psum.tile([P, N], F32, name="idle_ps", tag="vt_ps")
+        for turn in range(8):
+            nc.tensor.matmul(idle_ps[:], zeros[:, block(0)], zeros[:], start=True, stop=True)
+
         identity32 = held.tile([P, P], F32, name="identity32")
         make_identity(nc, identity32[:])
         identity = held.tile([P, P], BF16, name="identity")

@@ -7,6 +7,7 @@ P = 128
 S, K, M, N, D = 512, 256, 128, 256, 256
 KB, NB, DB = K // P, N // P, D // P
 LANES = 16
+WARM_UPS = 12
 FLOPS = 2 * K * N * (2 * M + D) + 2 * N * N * (M + D)
 BYTES = 2 * K * N + 2 * K * (2 * M + D) + 4 * N + 2 * P * (N // LANES) + 4 * N * D
 
@@ -17,6 +18,10 @@ ACT = mybir.ActivationFunctionType
 
 def block(b):
     return slice(b * P, (b + 1) * P)
+
+
+def deal_keys(copy, dealt, bank):
+    copy(dealt[:].rearrange("m (j p) -> m j p", j=NB), bank[:].rearrange("m (p j) -> m j p", j=NB))
 
 
 def tile_rows_pruneattn_sub_kernel(tc, table, qw, kw, w, r, offs, out):
@@ -33,32 +38,26 @@ def tile_rows_pruneattn_sub_kernel(tc, table, qw, kw, w, r, offs, out):
         offsets = held.tile([P, N // LANES], U16, name="offsets")
         bias = held.tile([P, NB], F32, name="bias")
         nc.sync.dma_start(offsets[:], offs)
+        nc.scalar.dma_start(bias[:], r.rearrange("o (p j) -> p (o j)", j=NB))
+        nc.sync.dma_start(qw_sb[:], qw.rearrange("(p a) m -> p a m", a=KB))
         nc.sync.dma_start(tokens[:], table.rearrange("(p a) s -> p a s", a=KB))
-        nc.scalar.dma_start(bias[:], r.rearrange("o (j p) -> p (o j)", p=P))
-        nc.scalar.dma_start(qw_sb[:], qw.rearrange("(p a) m -> p a m", a=KB))
         nc.scalar.dma_start(kw_sb[:], kw.rearrange("(p a) m -> p a m", a=KB))
         nc.sync.dma_start(w_sb[:], w.rearrange("(p a) d -> p a d", a=KB))
+
+        zeros = held.tile([P, P], BF16, name="zeros")
+        nc.vector.memset(zeros[:], 0.0)
+        idle_ps = psum.tile([P, P], F32, name="idle_ps", tag="vt_ps")
+        for turn in range(WARM_UPS):
+            nc.tensor.matmul(idle_ps[:], zeros[:], zeros[:], start=True, stop=True)
 
         warm = held.tile([P, 1], F32, name="warm")
         nc.vector.memset(warm[:], 0.0)
         nc.scalar.activation(warm[:], warm[:], ACT.Exp)
 
-        zeros = held.tile([P, N], BF16, name="zeros")
-        nc.gpsimd.memset(zeros[:], 0.0)
-        idle_ps = psum.tile([P, N], F32, name="idle_ps", tag="vt_ps")
-        for turn in range(8):
-            nc.tensor.matmul(idle_ps[:], zeros[:, block(0)], zeros[:], start=True, stop=True)
-
         identity32 = held.tile([P, P], F32, name="identity32")
         make_identity(nc, identity32[:])
         identity = held.tile([P, P], BF16, name="identity")
         nc.vector.tensor_copy(identity[:], identity32[:])
-
-        scores = [psum.tile([P, N], F32, name=f"scores{i}", tag="scores") for i in range(NB)]
-        for i in range(NB):
-            for j in range(NB):
-                nc.tensor.matmul(scores[i][:, block(j)], bias[:, j:j + 1].to_broadcast([P, P]), identity32[:],
-                                 start=(j == 0), stop=False, is_transpose=True)
 
         def project(weights, columns, name, tag):
             bank = psum.tile([P, N], F32, name=name, tag=tag)
@@ -67,18 +66,22 @@ def tile_rows_pruneattn_sub_kernel(tc, table, qw, kw, w, r, offs, out):
                                  start=(a == 0), stop=(a == KB - 1))
             return bank
 
-        q_ps = project(qw_sb, block(0), "q_ps", "qk_then_p")
-        h_ps = project(kw_sb, block(0), "h_ps", "qk_then_p")
+        q_ps = project(qw_sb, block(0), "q_ps", "qh_then_pt")
+        h_ps = project(kw_sb, block(0), "h_ps", "qh_then_pt")
         v_ps = [project(w_sb, block(d), f"v_ps{d}", "v_then_out") for d in range(DB)]
 
         q_sb = held.tile([P, N], BF16, name="q_sb")
         h_sb = held.tile([P, N], BF16, name="h_sb")
         nc.vector.tensor_scalar(q_sb[:], q_ps[:], 1.0 / math.sqrt(M), None, ALU.mult)
-        nc.vector.tensor_copy(h_sb[:], h_ps[:])
+        deal_keys(nc.vector.tensor_copy, h_sb, h_ps)
 
+        score_tags = ("scores_then_out", "qh_then_pt")
+        scores = [psum.tile([P, N], F32, name=f"scores{i}", tag=score_tags[i]) for i in range(NB)]
         for i in range(NB):
+            for j in range(NB):
+                nc.tensor.matmul(scores[i][:, block(j)], bias[:, j:j + 1].to_broadcast([P, P]), identity32[:],
+                                 start=(j == 0), stop=False, is_transpose=True)
             nc.tensor.matmul(scores[i][:], q_sb[:, block(i)], h_sb[:], start=False, stop=True)
-
         shifts = []
         for i in range(NB):
             shift = work.tile([P, 1], F32, name="shift")
@@ -88,12 +91,13 @@ def tile_rows_pruneattn_sub_kernel(tc, table, qw, kw, w, r, offs, out):
         vt_sb = held.tile([P, NB, D], BF16, name="vt_sb")
         for d in range(DB):
             v_sb = work.tile([P, N], BF16, name="v_sb")
-            nc.scalar.copy(v_sb[:], v_ps[d][:])
+            deal_keys(nc.scalar.copy, v_sb, v_ps[d])
             vt_ps = psum.tile([P, NB, P], BF16, name="vt_ps")
             for j in range(NB):
                 nc.tensor.transpose(vt_ps[:, j, :], v_sb[:, block(j)], identity[:])
             nc.vector.tensor_copy(vt_sb[:, :, block(d)], vt_ps[:])
 
+        out_tags = ("v_then_out", "scores_then_out")
         for i in range(NB):
             p_sb = work.tile([P, N], BF16, name="p_sb")
             total = work.tile([P, 1], F32, name="total")
@@ -101,20 +105,21 @@ def tile_rows_pruneattn_sub_kernel(tc, table, qw, kw, w, r, offs, out):
             inverse = work.tile([P, 1], F32, name="inverse")
             nc.vector.reciprocal(inverse[:], total[:])
 
-            pt_ps = psum.tile([P, NB, P], BF16, name="pt_ps", tag="qk_then_p")
+            pt_ps = psum.tile([P, NB, P], BF16, name="pt_ps", tag="qh_then_pt")
             for j in range(NB):
                 nc.tensor.transpose(pt_ps[:, j, :], p_sb[:, block(j)], identity[:])
             pt_sb = work.tile([P, NB, P], BF16, name="pt_sb")
-            out_ps = psum.tile([P, D], F32, name="out_ps", tag="v_then_out")
-            out_sb = work.tile([P, D], F32, name="out_sb")
-            if i % 2 == 0:
+            if i < NB - 1:
                 nc.vector.tensor_copy(pt_sb[:], pt_ps[:])
             else:
                 nc.scalar.copy(pt_sb[:], pt_ps[:])
-            for j in range(NB):
-                nc.tensor.matmul(out_ps[:], pt_sb[:, j, :], vt_sb[:, j, :], start=(j == 0), stop=(j == NB - 1))
-            if i % 2 == 0:
-                nc.vector.tensor_scalar(out_sb[:], out_ps[:], inverse[:], None, ALU.mult)
-            else:
-                nc.scalar.activation(out_sb[:], out_ps[:], ACT.Copy, scale=inverse[:])
+
+            halves = [psum.tile([P, P], F32, name=f"out_ps{d}", tag=out_tags[d]) for d in range(DB)]
+            for d in range(DB):
+                for j in range(NB):
+                    nc.tensor.matmul(halves[d][:], pt_sb[:, j, :], vt_sb[:, j, block(d)],
+                                     start=(j == 0), stop=(j == NB - 1))
+            out_sb = work.tile([P, D], F32, name="out_sb")
+            nc.scalar.activation(out_sb[:, block(0)], halves[0][:], ACT.Copy, scale=inverse[:])
+            nc.vector.tensor_scalar(out_sb[:, block(1)], halves[1][:], inverse[:], None, ALU.mult)
             nc.sync.dma_start(out[block(i), :], out_sb[:])

import math

import concourse.mybir as mybir
from concourse.masks import make_identity

P = 128
S, K, M, N, D = 512, 256, 128, 256, 256
KB, NB, DB = K // P, N // P, D // P
LANES = 16
WARM_UPS = 12
FLOPS = 2 * K * N * (2 * M + D) + 2 * N * N * (M + D)
BYTES = 2 * K * N + 2 * K * (2 * M + D) + 4 * N + 2 * P * (N // LANES) + 4 * N * D

BF16, F32, U16 = mybir.dt.bfloat16, mybir.dt.float32, mybir.dt.uint16
ALU = mybir.AluOpType
ACT = mybir.ActivationFunctionType


def block(b):
    return slice(b * P, (b + 1) * P)


def deal_keys(copy, dealt, bank):
    copy(dealt[:].rearrange("m (j p) -> m j p", j=NB), bank[:].rearrange("m (p j) -> m j p", j=NB))


def tile_rows_pruneattn_sub_kernel(tc, table, qw, kw, w, r, offs, out):
    nc = tc.nc
    with (
        tc.tile_pool(name="held", bufs=1) as held,
        tc.tile_pool(name="work", bufs=NB) as work,
        tc.psum_pool(name="psum", bufs=2) as psum,
    ):
        tokens = held.tile([P, KB, S], BF16, name="tokens")
        qw_sb = held.tile([P, KB, M], BF16, name="qw_sb")
        kw_sb = held.tile([P, KB, M], BF16, name="kw_sb")
        w_sb = held.tile([P, KB, D], BF16, name="w_sb")
        offsets = held.tile([P, N // LANES], U16, name="offsets")
        bias = held.tile([P, NB], F32, name="bias")
        nc.sync.dma_start(offsets[:], offs)
        nc.scalar.dma_start(bias[:], r.rearrange("o (p j) -> p (o j)", j=NB))
        nc.sync.dma_start(qw_sb[:], qw.rearrange("(p a) m -> p a m", a=KB))
        nc.sync.dma_start(tokens[:], table.rearrange("(p a) s -> p a s", a=KB))
        nc.scalar.dma_start(kw_sb[:], kw.rearrange("(p a) m -> p a m", a=KB))
        nc.sync.dma_start(w_sb[:], w.rearrange("(p a) d -> p a d", a=KB))

        zeros = held.tile([P, P], BF16, name="zeros")
        nc.vector.memset(zeros[:], 0.0)
        idle_ps = psum.tile([P, P], F32, name="idle_ps", tag="vt_ps")
        for turn in range(WARM_UPS):
            nc.tensor.matmul(idle_ps[:], zeros[:], zeros[:], start=True, stop=True)

        warm = held.tile([P, 1], F32, name="warm")
        nc.vector.memset(warm[:], 0.0)
        nc.scalar.activation(warm[:], warm[:], ACT.Exp)

        identity32 = held.tile([P, P], F32, name="identity32")
        make_identity(nc, identity32[:])
        identity = held.tile([P, P], BF16, name="identity")
        nc.vector.tensor_copy(identity[:], identity32[:])

        def project(weights, columns, name, tag):
            bank = psum.tile([P, N], F32, name=name, tag=tag)
            for a in range(KB):
                nc.tensor.matmul(bank[:], weights[:, a, columns], tokens[:, a, :].indirect(offsets[:]),
                                 start=(a == 0), stop=(a == KB - 1))
            return bank

        q_ps = project(qw_sb, block(0), "q_ps", "qh_then_pt")
        h_ps = project(kw_sb, block(0), "h_ps", "qh_then_pt")
        v_ps = [project(w_sb, block(d), f"v_ps{d}", "v_then_out") for d in range(DB)]

        q_sb = held.tile([P, N], BF16, name="q_sb")
        h_sb = held.tile([P, N], BF16, name="h_sb")
        nc.vector.tensor_scalar(q_sb[:], q_ps[:], 1.0 / math.sqrt(M), None, ALU.mult)
        deal_keys(nc.vector.tensor_copy, h_sb, h_ps)

        score_tags = ("scores_then_out", "qh_then_pt")
        scores = [psum.tile([P, N], F32, name=f"scores{i}", tag=score_tags[i]) for i in range(NB)]
        for i in range(NB):
            for j in range(NB):
                nc.tensor.matmul(scores[i][:, block(j)], bias[:, j:j + 1].to_broadcast([P, P]), identity32[:],
                                 start=(j == 0), stop=False, is_transpose=True)
            nc.tensor.matmul(scores[i][:], q_sb[:, block(i)], h_sb[:], start=False, stop=True)
        shifts = []
        for i in range(NB):
            shift = work.tile([P, 1], F32, name="shift")
            nc.vector.tensor_reduce(shift[:], scores[i][:], mybir.AxisListType.X, ALU.max, negate=True)
            shifts.append(shift)

        vt_sb = held.tile([P, NB, D], BF16, name="vt_sb")
        for d in range(DB):
            v_sb = work.tile([P, N], BF16, name="v_sb")
            deal_keys(nc.scalar.copy, v_sb, v_ps[d])
            vt_ps = psum.tile([P, NB, P], BF16, name="vt_ps")
            for j in range(NB):
                nc.tensor.transpose(vt_ps[:, j, :], v_sb[:, block(j)], identity[:])
            nc.vector.tensor_copy(vt_sb[:, :, block(d)], vt_ps[:])

        out_tags = ("v_then_out", "scores_then_out")
        for i in range(NB):
            p_sb = work.tile([P, N], BF16, name="p_sb")
            total = work.tile([P, 1], F32, name="total")
            nc.scalar.activation(p_sb[:], scores[i][:], ACT.Exp, bias=shifts[i][:], accum_out=total[:])
            inverse = work.tile([P, 1], F32, name="inverse")
            nc.vector.reciprocal(inverse[:], total[:])

            pt_ps = psum.tile([P, NB, P], BF16, name="pt_ps", tag="qh_then_pt")
            for j in range(NB):
                nc.tensor.transpose(pt_ps[:, j, :], p_sb[:, block(j)], identity[:])
            pt_sb = work.tile([P, NB, P], BF16, name="pt_sb")
            if i < NB - 1:
                nc.vector.tensor_copy(pt_sb[:], pt_ps[:])
            else:
                nc.scalar.copy(pt_sb[:], pt_ps[:])

            halves = [psum.tile([P, P], F32, name=f"out_ps{d}", tag=out_tags[d]) for d in range(DB)]
            for d in range(DB):
                for j in range(NB):
                    nc.tensor.matmul(halves[d][:], pt_sb[:, j, :], vt_sb[:, j, block(d)],
                                     start=(j == 0), stop=(j == NB - 1))
            out_sb = work.tile([P, D], F32, name="out_sb")
            nc.scalar.activation(out_sb[:, block(0)], halves[0][:], ACT.Copy, scale=inverse[:])
            nc.vector.tensor_scalar(out_sb[:, block(1)], halves[1][:], inverse[:], None, ALU.mult)
            nc.sync.dma_start(out[block(i), :], out_sb[:])
